import numpy as np
import ml_dtypes


def mxq(x, axis, fmt="e4m3"):
    dtype, down = {"e4m3": (ml_dtypes.float8_e4m3fn, 7), "e5m2": (ml_dtypes.float8_e5m2, 14)}[fmt]
    v = np.moveaxis(np.asarray(x, np.float32).astype(ml_dtypes.bfloat16).astype(np.float64), axis, -1)
    blocks = v.reshape(v.shape[:-1] + (-1, 32))
    amax = np.abs(blocks).max(-1, keepdims=True)
    byte = np.maximum(np.where(amax > 0, np.frexp(amax)[1] - 1 + 127, 0) - down, 1)
    scale = np.exp2(byte - 127.0)
    codes = (blocks / scale).astype(np.float32).astype(dtype).astype(np.float64)
    return np.moveaxis((codes * scale).reshape(v.shape), -1, axis)


WIDE = False


def mx_kscale(k):
    if not WIDE:
        return np.ones(k)
    levels = np.array([10, -10, 5, -5, 0])
    if k % 512:
        return np.exp2(np.random.permutation(np.resize(levels, k // 32))).repeat(32)
    a = np.empty((k // 512, 16))
    for p in range(k // 512):
        a[p, :8] = np.random.permutation(np.resize(levels, 8))
        for g in range(8):
            far = levels[np.abs(levels - a[p, g]) >= 10]
            a[p, g + 8] = far[np.random.randint(len(far))]
    return np.exp2(a.ravel()).repeat(32)


def f64(x):
    return np.asarray(x).astype(np.float64)


def striped(idx):
    return np.tile(np.asarray(idx).reshape(-1, 16).T, (8, 1)).astype(np.uint16)


def unstriped(offs):
    return offs[:16].T.reshape(-1).astype(np.int64)


E2M1 = np.array([0.0, 0.5, 1.0, 1.5, 2.0, 3.0, 4.0, 6.0, -0.0, -0.5, -1.0, -1.5, -2.0, -3.0, -4.0, -6.0])


def pack_weight(w, fmt):
    k, n = w.shape
    w = f64(np.asarray(w, np.float32).astype(ml_dtypes.bfloat16)).reshape(k // 32, 32, n)
    amax = np.abs(w).max(1)
    if fmt == "e4m3":
        byte = np.frexp(amax)[1] - 1 + 127 - 7
    else:
        mant, ex = np.frexp(amax / 6.0)
        byte = np.where(mant > 0.5, ex, ex - 1) + 127
    byte = np.clip(np.where(amax > 0, byte, 1), 1, 254)
    scaled = (w * np.exp2(127.0 - byte)[:, None, :]).reshape(k, n).astype(np.float32)
    by_word = np.ascontiguousarray(scaled.reshape(k // 512, 128, 4, n).transpose(0, 1, 3, 2))
    if fmt == "e4m3":
        words = by_word.astype(ml_dtypes.float8_e4m3fn).view(np.uint8)
    else:
        c = by_word.astype(ml_dtypes.float4_e2m1fn).view(np.uint8) & 0xF
        words = (c[..., 0::2] | (c[..., 1::2] << 4)).reshape(k // 512, 128, 2 * n)
    return np.ascontiguousarray(words), np.ascontiguousarray(byte.astype(np.uint8).reshape(k // 512, 16, n))


def unpack_weight(words, scales, fmt):
    g, _, n = scales.shape
    words = np.ascontiguousarray(words).reshape(g, 128, n, -1)
    if fmt == "e4m3":
        vals = words.view(ml_dtypes.float8_e4m3fn).astype(np.float64)
    else:
        nib = np.empty((g, 128, n, 4), np.uint8)
        nib[..., 0::2] = words & 0xF
        nib[..., 1::2] = words >> 4
        vals = E2M1[nib]
    vals = vals * np.repeat(np.exp2(scales.astype(np.float64) - 127.0), 8, axis=1)[..., None]
    return vals.transpose(0, 1, 3, 2).reshape(g * 512, n)


D, E, T, I, Q = 512, 512, 2048, 512, 128


def setup_inputs():
    n = np.random.standard_normal
    idx = np.random.permutation(T)[:I]
    fd = mx_kscale(D)
    fe = mx_kscale(E)
    keysp = pack_weight(n((D, T)) / fd[:, None], "e2m1")
    valsp = pack_weight(n((E, T)) / fe[:, None], "e2m1")
    return {
        "query": (n((D, Q)) * 0.7 / np.sqrt(D) * fd[:, None]).astype(np.float32),
        "keys_words": keysp[0],
        "keys_scales": keysp[1],
        "gout": (n((E, Q)) * 1 / np.sqrt(E) * fe[:, None]).astype(np.float32),
        "vals_words": valsp[0],
        "vals_scales": valsp[1],
        "dquery": (n((D, Q)) * 1.0 / np.sqrt(D) * fd[:, None]).astype(np.float32),
        "base": (0.5 * n((Q, T))).astype(np.float32),
        "offs": striped(idx),
    }


def reference(query, keys_words, keys_scales, gout, vals_words, vals_scales, dquery, base, offs):
    idx = unstriped(offs)
    keysu = unpack_weight(keys_words, keys_scales, "e2m1")
    valsu = unpack_weight(vals_words, vals_scales, "e2m1")
    queryq = mxq(f64(query), 0, "e4m3")
    keysidxg = keysu[:, idx]
    a = queryq.T @ keysidxg
    dqueryq = mxq(f64(dquery), 0, "e4m3")
    ta = dqueryq.T @ keysidxg
    p = np.exp(a - np.max(a, axis=1, keepdims=True))
    n2 = np.sqrt(np.sum(np.square(p), axis=1, keepdims=True))
    goutq = mxq(f64(gout), 0, "e4m3")
    valsidxg = valsu[:, idx]
    c0 = goutq.T @ valsidxg
    dn2 = np.sum(c0 * p / np.square(n2) * (-1.0), axis=1, keepdims=True)
    dp = c0 / n2 + dn2 * 0.5 / np.sqrt(np.sum(np.square(p), axis=1, keepdims=True)) * p * 2.0
    tp = ta * p
    tn2 = np.sum(tp * p * 2.0, axis=1, keepdims=True) * 0.5 / n2
    tdn2 = np.sum((tp * c0 - tn2 * n2 * 2.0 * c0 * p / np.square(n2)) / np.square(n2) * (-1.0), axis=1, keepdims=True)
    tdp = tn2 * c0 / np.square(n2) * (-1.0) + ((tdn2 * 0.5 - np.sum(tp * p * 2.0, axis=1, keepdims=True) * 0.5 / np.sqrt(np.sum(np.square(p), axis=1, keepdims=True)) * dn2 * 0.5 / np.sqrt(np.sum(np.square(p), axis=1, keepdims=True))) / np.sqrt(np.sum(np.square(p), axis=1, keepdims=True)) * p + tp * dn2 * 0.5 / np.sqrt(np.sum(np.square(p), axis=1, keepdims=True))) * 2.0
    tda = tdp * p + tp * dp
    gs = tda * 16.0
    gf = np.zeros((Q, T))
    gf[:, idx] = gs
    y = f64(base) + gf
    return y

@@ -1,0 +1,180 @@
+from contextlib import ExitStack
+
+import concourse.mybir as mybir
+
+F32 = mybir.dt.float32
+BF16 = mybir.dt.bfloat16
+I32 = mybir.dt.int32
+U32 = mybir.dt.uint32
+U16 = mybir.dt.uint16
+U8 = mybir.dt.uint8
+FP8X4 = mybir.dt.float8_e4m3fn_x4
+FP4X4 = mybir.dt.float4_e2m1fn_x4
+ALU = mybir.AluOpType
+ACT = mybir.ActivationFunctionType
+
+P = 128
+PACK = 4
+FEATURES = 512
+TOKENS = 2048
+SLOTS = 512
+ROWS = 128
+OUT_WIDTHS = (512, 512, 512, 512)
+
+FLOPS = 3 * 2 * FEATURES * ROWS * SLOTS
+
+
+def tile_attend_hvunitweights_s_kernel(
+    tc, query, keys_words, keys_scales, gout, vals_words, vals_scales, dquery, base, offs, out
+):
+    nc = tc.nc
+    with ExitStack() as ctx:
+        held = ctx.enter_context(tc.tile_pool(name="held", bufs=1))
+        psum = ctx.enter_context(tc.psum_pool(name="psum", bufs=1))
+
+        offsets = held.tile([P, SLOTS // 16], U16, name="offsets")
+        nc.sync.dma_start(offsets[:], offs)
+
+        def load_scales(src, name):
+            plane = held.tile([P, TOKENS], U8, name=name, tag=name, align_bytes=64)
+            nc.gpsimd.memset(plane[:].bitcast(I32)[:, 0:256], 0)
+            nc.vector.memset(plane[:].bitcast(I32)[:, 256:512], 0)
+            rows = src[0].bitcast(I32).rearrange("(q r) c -> r q c", r=4)
+            for r in range(4):
+                nc.sync.dma_start(plane[r:P:32, :].bitcast(I32), rows[r])
+            return plane
+
+        def load_words(src, name):
+            words = held.tile([P, TOKENS], U16, name=name, align_bytes=64)
+            nc.sync.dma_start(words[:].bitcast(I32), src[0].bitcast(I32))
+            return words
+
+        def load_rows(src, name):
+            raw = held.tile([P, PACK, ROWS], F32, name=name, tag=name, align_bytes=64)
+            nc.sync.dma_start(raw[:], src.rearrange("(p j) w -> p j w", j=PACK))
+            return raw
+
+        def gather(window, dtype, name, tag):
+            picked = held.tile([P, SLOTS], dtype, name=name, tag=tag, align_bytes=64)
+            nc.vector.tensor_copy(picked[:], window[:].indirect(offsets[:]))
+            return picked
+
+        def interleave(raw, name):
+            grouped = held.tile([P, ROWS, PACK], BF16, name=name, tag=name, align_bytes=64)
+            nc.scalar.activation(
+                grouped[:].rearrange("p (c i) t -> p c t i", i=4),
+                raw[:].rearrange("p t (c i) -> p c t i", i=4),
+                ACT.Copy,
+            )
+            return grouped
+
+        def quantize(grouped, name, tag):
+            codes = held.tile([P, ROWS], U32, name=name + "_codes", tag=tag, align_bytes=64)
+            scales = held.tile([P, ROWS], U8, name=name + "_scales", align_bytes=64)
+            nc.vector.quantize_mx(
+                out=codes[:].bitcast(FP8X4),
+                scales=scales[:],
+                in_=grouped[:].rearrange("p w j -> p (w j)"),
+            )
+            return codes, scales
+
+        def product(rows_mx, words, scales, name):
+            acc = psum.tile([ROWS, SLOTS], F32, name=name)
+            nc.tensor.matmul_mx(
+                out=acc[:],
+                lhsT=rows_mx[0][:].bitcast(FP8X4),
+                lhsT_scale=rows_mx[1][:],
+                rhs=words[:].bitcast(FP4X4),
+                rhs_scale=scales[:],
+                start=True,
+                stop=True,
+            )
+            return acc
+
+        def column(name, width=1):
+            return held.tile([P, width], F32, name=name)
+
+        def wide(name):
+            return held.tile([P, SLOTS], F32, name=name)
+
+        key_word_pool = load_words(keys_words, "key_word_pool")
+        key_scale_pool = load_scales(keys_scales, "key_scale_pool")
+        query_raw = load_rows(query, "query_raw")
+        val_word_pool = load_words(vals_words, "val_word_pool")
+        dquery_raw = load_rows(dquery, "dquery_raw")
+        val_scale_pool = load_scales(vals_scales, "val_scale_pool")
+        gout_raw = load_rows(gout, "gout_raw")
+        base_sb = held.tile([P, TOKENS], F32, name="base_sb")
+        nc.sync.dma_start(base_sb[:], base)
+
+        placed = held.tile([P, TOKENS], F32, name="placed")
+        nc.vector.memset(placed[:], 0.0)
+        beta_factors = column("beta_factors", 2)
+        nc.gpsimd.memset(beta_factors[:, 0:1], -0.5)
+        nc.gpsimd.memset(beta_factors[:, 1:2], -1.0)
+
+        query_bf = interleave(query_raw, "query_bf")
+        dquery_bf = interleave(dquery_raw, "dquery_bf")
+        gout_bf = interleave(gout_raw, "gout_bf")
+
+        key_words = gather(key_word_pool, U16, "key_words", "key_words")
+        key_scales = gather(key_scale_pool, U8, "key_scales", "key_scales")
+        query_mx = quantize(query_bf, "query", "query_codes")
+        a = product(query_mx, key_words, key_scales, "a")
+        val_words = gather(val_word_pool, U16, "val_words", "query_raw")
+
+        minus_2a = wide("minus_2a")
+        minus_2max = column("minus_2max")
+        nc.vector.tensor_scalar(minus_2a[:], a[:], -2.0, None, ALU.mult, ALU.min, accum_out=minus_2max[:])
+        v = held.tile([P, SLOTS], F32, name="v", tag="gout_raw", align_bytes=64)
+        s = column("s")
+        nc.scalar.activation(v[:], minus_2a[:], ACT.Exp, bias=minus_2max[:], scale=-1.0, accum_out=s[:])
+        minus_max = column("minus_max")
+        nc.scalar.activation(minus_max[:], minus_2max[:], ACT.Copy, scale=0.5)
+        p = wide("p")
+        nc.scalar.activation(p[:], minus_2a[:], ACT.Exp, bias=minus_max[:], scale=-0.5)
+
+        dquery_mx = quantize(dquery_bf, "dquery", "dquery_codes")
+        ta = product(dquery_mx, key_words, key_scales, "ta")
+        val_scales = gather(val_scale_pool, U8, "val_scales", "dquery_raw")
+        gout_mx = quantize(gout_bf, "gout", "gout_codes")
+        c0 = product(gout_mx, val_words, val_scales, "c0")
+
+        powers = column("powers", 2)
+        nc.gpsimd.tensor_tensor(powers[:], s[:].to_broadcast([P, 2]), beta_factors[:], ALU.pow)
+        inv_s = powers[:, 1:2]
+        out_scale = column("out_scale")
+        nc.scalar.activation(out_scale[:], powers[:, 0:1], ACT.Copy, scale=-16.0)
+
+        tv2 = wide("tv2")
+        b2 = column("b2")
+        nc.vector.scalar_tensor_tensor(tv2[:], ta[:], 2.0, v[:], ALU.mult, ALU.mult, accum_out=b2[:])
+        u = wide("u")
+        sum_u = column("sum_u")
+        nc.vector.scalar_tensor_tensor(u[:], c0[:], 1.0, p[:], ALU.mult, ALU.mult, accum_out=sum_u[:])
+        minus_beta = column("minus_beta", 2)
+        nc.vector.tensor_scalar(minus_beta[:], beta_factors[:], b2[:], inv_s, ALU.mult, ALU.mult)
+        y = wide("y")
+        sum_y = column("sum_y")
+        nc.vector.scalar_tensor_tensor(y[:], ta[:], minus_beta[:, 0:1], u[:], ALU.add, ALU.mult, accum_out=sum_y[:])
+
+        alpha = column("alpha")
+        nc.scalar.activation(alpha[:], sum_u[:], ACT.Copy, scale=inv_s)
+        cross = column("cross")
+        nc.scalar.activation(cross[:], alpha[:], ACT.Copy, scale=minus_beta[:, 1:2])
+        tv_term = wide("tv_term")
+        nc.scalar.activation(tv_term[:], tv2[:], ACT.Copy, scale=alpha[:])
+
+        v_factor = column("v_factor")
+        nc.vector.tensor_scalar(v_factor[:], sum_y[:], inv_s, cross[:], ALU.mult, ALU.add)
+        rest = wide("rest")
+        nc.vector.scalar_tensor_tensor(rest[:], v[:], v_factor[:], y[:], ALU.mult, ALU.subtract)
+        nc.vector.tensor_tensor(placed[:].indirect(offsets[:]), rest[:], tv_term[:], ALU.add)
+
+        start = 0
+        for n, width in enumerate(OUT_WIDTHS):
+            cols = slice(start, start + width)
+            result = held.tile([P, width], F32, name="result%d" % n)
+            nc.vector.scalar_tensor_tensor(result[:], placed[:, cols], out_scale[:], base_sb[:, cols], ALU.mult, ALU.add)
+            nc.sync.dma_start(out[:, cols], result[:])
+            start = start + width

@@ -19,7 +19,7 @@ FEATURES = 512
 TOKENS = 2048
 SLOTS = 512
 ROWS = 128
-OUT_WIDTHS = (512, 512, 512, 512)
+OUT_WIDTHS = (256, 512, 512, 512, 256)
 
 FLOPS = 3 * 2 * FEATURES * ROWS * SLOTS
 
@@ -126,13 +126,14 @@ def tile_attend_hvunitweights_s_kernel(
         minus_2a = wide("minus_2a")
         minus_2max = column("minus_2max")
         nc.vector.tensor_scalar(minus_2a[:], a[:], -2.0, None, ALU.mult, ALU.min, accum_out=minus_2max[:])
-        v = held.tile([P, SLOTS], F32, name="v", tag="gout_raw", align_bytes=64)
+        v_and_max = held.tile([P, SLOTS + 8], F32, name="v_and_max", tag="gout_raw", align_bytes=64)
+        v = v_and_max[:, 0:SLOTS]
+        minus_max = v_and_max[:, SLOTS : SLOTS + 1]
         s = column("s")
-        nc.scalar.activation(v[:], minus_2a[:], ACT.Exp, bias=minus_2max[:], scale=-1.0, accum_out=s[:])
-        minus_max = column("minus_max")
-        nc.scalar.activation(minus_max[:], minus_2max[:], ACT.Copy, scale=0.5)
+        nc.scalar.activation(v, minus_2a[:], ACT.Exp, bias=minus_2max[:], scale=-1.0, accum_out=s[:])
+        nc.scalar.activation(minus_max, minus_2max[:], ACT.Copy, scale=0.5)
         p = wide("p")
-        nc.scalar.activation(p[:], minus_2a[:], ACT.Exp, bias=minus_max[:], scale=-0.5)
+        nc.scalar.activation(p[:], minus_2a[:], ACT.Exp, bias=minus_max, scale=-0.5)
 
         dquery_mx = quantize(dquery_bf, "dquery", "dquery_codes")
         ta = product(dquery_mx, key_words, key_scales, "ta")
@@ -148,12 +149,14 @@ def tile_attend_hvunitweights_s_kernel(
 
         tv2 = wide("tv2")
         b2 = column("b2")
-        nc.vector.scalar_tensor_tensor(tv2[:], ta[:], 2.0, v[:], ALU.mult, ALU.mult, accum_out=b2[:])
+        nc.vector.scalar_tensor_tensor(tv2[:], ta[:], 2.0, v, ALU.mult, ALU.mult, accum_out=b2[:])
         u = wide("u")
         sum_u = column("sum_u")
         nc.vector.scalar_tensor_tensor(u[:], c0[:], 1.0, p[:], ALU.mult, ALU.mult, accum_out=sum_u[:])
+        factors_over_s = column("factors_over_s", 2)
+        nc.scalar.activation(factors_over_s[:], beta_factors[:], ACT.Copy, scale=inv_s)
         minus_beta = column("minus_beta", 2)
-        nc.vector.tensor_scalar(minus_beta[:], beta_factors[:], b2[:], inv_s, ALU.mult, ALU.mult)
+        nc.scalar.activation(minus_beta[:], factors_over_s[:], ACT.Copy, scale=b2[:])
         y = wide("y")
         sum_y = column("sum_y")
         nc.vector.scalar_tensor_tensor(y[:], ta[:], minus_beta[:, 0:1], u[:], ALU.add, ALU.mult, accum_out=sum_y[:])
@@ -168,7 +171,7 @@ def tile_attend_hvunitweights_s_kernel(
         v_factor = column("v_factor")
         nc.vector.tensor_scalar(v_factor[:], sum_y[:], inv_s, cross[:], ALU.mult, ALU.add)
         rest = wide("rest")
-        nc.vector.scalar_tensor_tensor(rest[:], v[:], v_factor[:], y[:], ALU.mult, ALU.subtract)
+        nc.vector.scalar_tensor_tensor(rest[:], v, v_factor[:], y[:], ALU.mult, ALU.subtract)
         nc.vector.tensor_tensor(placed[:].indirect(offsets[:]), rest[:], tv_term[:], ALU.add)
 
         start = 0

@@ -33,7 +33,6 @@ def tile_attend_hvunitweights_s_kernel(
         psum = ctx.enter_context(tc.psum_pool(name="psum", bufs=1))
 
         offsets = held.tile([P, SLOTS // 16], U16, name="offsets")
-        nc.sync.dma_start(offsets[:], offs)
 
         def load_scales(src, name):
             plane = held.tile([P, TOKENS], U8, name=name, tag=name, align_bytes=64)
@@ -98,12 +97,13 @@ def tile_attend_hvunitweights_s_kernel(
             return held.tile([P, SLOTS], F32, name=name)
 
         key_word_pool = load_words(keys_words, "key_word_pool")
+        nc.sync.dma_start(offsets[:], offs)
         key_scale_pool = load_scales(keys_scales, "key_scale_pool")
         query_raw = load_rows(query, "query_raw")
-        val_word_pool = load_words(vals_words, "val_word_pool")
-        dquery_raw = load_rows(dquery, "dquery_raw")
         val_scale_pool = load_scales(vals_scales, "val_scale_pool")
+        dquery_raw = load_rows(dquery, "dquery_raw")
         gout_raw = load_rows(gout, "gout_raw")
+        val_word_pool = load_words(vals_words, "val_word_pool")
         base_sb = held.tile([P, TOKENS], F32, name="base_sb")
         nc.sync.dma_start(base_sb[:], base)
 
@@ -121,7 +121,7 @@ def tile_attend_hvunitweights_s_kernel(
         key_scales = gather(key_scale_pool, U8, "key_scales", "key_scales")
         query_mx = quantize(query_bf, "query", "query_codes")
         a = product(query_mx, key_words, key_scales, "a")
-        val_words = gather(val_word_pool, U16, "val_words", "query_raw")
+        val_scales = gather(val_scale_pool, U8, "val_scales", "query_raw")
 
         minus_2a = wide("minus_2a")
         minus_2max = column("minus_2max")
@@ -137,9 +137,23 @@ def tile_attend_hvunitweights_s_kernel(
 
         dquery_mx = quantize(dquery_bf, "dquery", "dquery_codes")
         ta = product(dquery_mx, key_words, key_scales, "ta")
-        val_scales = gather(val_scale_pool, U8, "val_scales", "dquery_raw")
         gout_mx = quantize(gout_bf, "gout", "gout_codes")
-        c0 = product(gout_mx, val_words, val_scales, "c0")
+        val_words = held.tile([P, SLOTS], U16, name="val_words", align_bytes=64)
+        c0 = psum.tile([ROWS, SLOTS], F32, name="c0")
+        half = SLOTS // 2
+        for h in range(2):
+            slots = slice(h * half, (h + 1) * half)
+            part = offsets[:, h * half // 16 : (h + 1) * half // 16]
+            nc.vector.tensor_copy(val_words[:, slots], val_word_pool[:].indirect(part))
+            nc.tensor.matmul_mx(
+                out=c0[:, slots],
+                lhsT=gout_mx[0][:].bitcast(FP8X4),
+                lhsT_scale=gout_mx[1][:],
+                rhs=val_words[:, slots].bitcast(FP4X4),
+                rhs_scale=val_scales[:, slots],
+                start=True,
+                stop=True,
+            )
 
         powers = column("powers", 2)
         nc.gpsimd.tensor_tensor(powers[:], s[:].to_broadcast([P, 2]), beta_factors[:], ALU.pow)

from contextlib import ExitStack

import concourse.mybir as mybir

F32 = mybir.dt.float32
BF16 = mybir.dt.bfloat16
I32 = mybir.dt.int32
U32 = mybir.dt.uint32
U16 = mybir.dt.uint16
U8 = mybir.dt.uint8
FP8X4 = mybir.dt.float8_e4m3fn_x4
FP4X4 = mybir.dt.float4_e2m1fn_x4
ALU = mybir.AluOpType
ACT = mybir.ActivationFunctionType

P = 128
PACK = 4
FEATURES = 512
TOKENS = 2048
SLOTS = 512
ROWS = 128
OUT_WIDTHS = (256, 512, 512, 512, 256)

FLOPS = 3 * 2 * FEATURES * ROWS * SLOTS


def tile_attend_hvunitweights_s_kernel(
    tc, query, keys_words, keys_scales, gout, vals_words, vals_scales, dquery, base, offs, out
):
    nc = tc.nc
    with ExitStack() as ctx:
        held = ctx.enter_context(tc.tile_pool(name="held", bufs=1))
        psum = ctx.enter_context(tc.psum_pool(name="psum", bufs=1))

        offsets = held.tile([P, SLOTS // 16], U16, name="offsets")

        def load_scales(src, name):
            plane = held.tile([P, TOKENS], U8, name=name, tag=name, align_bytes=64)
            nc.gpsimd.memset(plane[:].bitcast(I32)[:, 0:256], 0)
            nc.vector.memset(plane[:].bitcast(I32)[:, 256:512], 0)
            rows = src[0].bitcast(I32).rearrange("(q r) c -> r q c", r=4)
            for r in range(4):
                nc.sync.dma_start(plane[r:P:32, :].bitcast(I32), rows[r])
            return plane

        def load_words(src, name):
            words = held.tile([P, TOKENS], U16, name=name, align_bytes=64)
            nc.sync.dma_start(words[:].bitcast(I32), src[0].bitcast(I32))
            return words

        def load_rows(src, name):
            raw = held.tile([P, PACK, ROWS], F32, name=name, tag=name, align_bytes=64)
            nc.sync.dma_start(raw[:], src.rearrange("(p j) w -> p j w", j=PACK))
            return raw

        def gather(window, dtype, name, tag):
            picked = held.tile([P, SLOTS], dtype, name=name, tag=tag, align_bytes=64)
            nc.vector.tensor_copy(picked[:], window[:].indirect(offsets[:]))
            return picked

        def interleave(raw, name):
            grouped = held.tile([P, ROWS, PACK], BF16, name=name, tag=name, align_bytes=64)
            nc.scalar.activation(
                grouped[:].rearrange("p (c i) t -> p c t i", i=4),
                raw[:].rearrange("p t (c i) -> p c t i", i=4),
                ACT.Copy,
            )
            return grouped

        def quantize(grouped, name, tag):
            codes = held.tile([P, ROWS], U32, name=name + "_codes", tag=tag, align_bytes=64)
            scales = held.tile([P, ROWS], U8, name=name + "_scales", align_bytes=64)
            nc.vector.quantize_mx(
                out=codes[:].bitcast(FP8X4),
                scales=scales[:],
                in_=grouped[:].rearrange("p w j -> p (w j)"),
            )
            return codes, scales

        def product(rows_mx, words, scales, name):
            acc = psum.tile([ROWS, SLOTS], F32, name=name)
            nc.tensor.matmul_mx(
                out=acc[:],
                lhsT=rows_mx[0][:].bitcast(FP8X4),
                lhsT_scale=rows_mx[1][:],
                rhs=words[:].bitcast(FP4X4),
                rhs_scale=scales[:],
                start=True,
                stop=True,
            )
            return acc

        def column(name, width=1):
            return held.tile([P, width], F32, name=name)

        def wide(name):
            return held.tile([P, SLOTS], F32, name=name)

        key_word_pool = load_words(keys_words, "key_word_pool")
        nc.sync.dma_start(offsets[:], offs)
        key_scale_pool = load_scales(keys_scales, "key_scale_pool")
        query_raw = load_rows(query, "query_raw")
        val_scale_pool = load_scales(vals_scales, "val_scale_pool")
        dquery_raw = load_rows(dquery, "dquery_raw")
        gout_raw = load_rows(gout, "gout_raw")
        val_word_pool = load_words(vals_words, "val_word_pool")
        base_sb = held.tile([P, TOKENS], F32, name="base_sb")
        nc.sync.dma_start(base_sb[:], base)

        placed = held.tile([P, TOKENS], F32, name="placed")
        nc.vector.memset(placed[:], 0.0)
        beta_factors = column("beta_factors", 2)
        nc.gpsimd.memset(beta_factors[:, 0:1], -0.5)
        nc.gpsimd.memset(beta_factors[:, 1:2], -1.0)

        query_bf = interleave(query_raw, "query_bf")
        dquery_bf = interleave(dquery_raw, "dquery_bf")
        gout_bf = interleave(gout_raw, "gout_bf")

        key_words = gather(key_word_pool, U16, "key_words", "key_words")
        key_scales = gather(key_scale_pool, U8, "key_scales", "key_scales")
        query_mx = quantize(query_bf, "query", "query_codes")
        a = product(query_mx, key_words, key_scales, "a")
        val_scales = gather(val_scale_pool, U8, "val_scales", "query_raw")

        minus_2a = wide("minus_2a")
        minus_2max = column("minus_2max")
        nc.vector.tensor_scalar(minus_2a[:], a[:], -2.0, None, ALU.mult, ALU.min, accum_out=minus_2max[:])
        v_and_max = held.tile([P, SLOTS + 8], F32, name="v_and_max", tag="gout_raw", align_bytes=64)
        v = v_and_max[:, 0:SLOTS]
        minus_max = v_and_max[:, SLOTS : SLOTS + 1]
        s = column("s")
        nc.scalar.activation(v, minus_2a[:], ACT.Exp, bias=minus_2max[:], scale=-1.0, accum_out=s[:])
        nc.scalar.activation(minus_max, minus_2max[:], ACT.Copy, scale=0.5)
        p = wide("p")
        nc.scalar.activation(p[:], minus_2a[:], ACT.Exp, bias=minus_max, scale=-0.5)

        dquery_mx = quantize(dquery_bf, "dquery", "dquery_codes")
        ta = product(dquery_mx, key_words, key_scales, "ta")
        gout_mx = quantize(gout_bf, "gout", "gout_codes")
        val_words = held.tile([P, SLOTS], U16, name="val_words", align_bytes=64)
        c0 = psum.tile([ROWS, SLOTS], F32, name="c0")
        half = SLOTS // 2
        for h in range(2):
            slots = slice(h * half, (h + 1) * half)
            part = offsets[:, h * half // 16 : (h + 1) * half // 16]
            nc.vector.tensor_copy(val_words[:, slots], val_word_pool[:].indirect(part))
            nc.tensor.matmul_mx(
                out=c0[:, slots],
                lhsT=gout_mx[0][:].bitcast(FP8X4),
                lhsT_scale=gout_mx[1][:],
                rhs=val_words[:, slots].bitcast(FP4X4),
                rhs_scale=val_scales[:, slots],
                start=True,
                stop=True,
            )

        powers = column("powers", 2)
        nc.gpsimd.tensor_tensor(powers[:], s[:].to_broadcast([P, 2]), beta_factors[:], ALU.pow)
        inv_s = powers[:, 1:2]
        out_scale = column("out_scale")
        nc.scalar.activation(out_scale[:], powers[:, 0:1], ACT.Copy, scale=-16.0)

        tv2 = wide("tv2")
        b2 = column("b2")
        nc.vector.scalar_tensor_tensor(tv2[:], ta[:], 2.0, v, ALU.mult, ALU.mult, accum_out=b2[:])
        u = wide("u")
        sum_u = column("sum_u")
        nc.vector.scalar_tensor_tensor(u[:], c0[:], 1.0, p[:], ALU.mult, ALU.mult, accum_out=sum_u[:])
        factors_over_s = column("factors_over_s", 2)
        nc.scalar.activation(factors_over_s[:], beta_factors[:], ACT.Copy, scale=inv_s)
        minus_beta = column("minus_beta", 2)
        nc.scalar.activation(minus_beta[:], factors_over_s[:], ACT.Copy, scale=b2[:])
        y = wide("y")
        sum_y = column("sum_y")
        nc.vector.scalar_tensor_tensor(y[:], ta[:], minus_beta[:, 0:1], u[:], ALU.add, ALU.mult, accum_out=sum_y[:])

        alpha = column("alpha")
        nc.scalar.activation(alpha[:], sum_u[:], ACT.Copy, scale=inv_s)
        cross = column("cross")
        nc.scalar.activation(cross[:], alpha[:], ACT.Copy, scale=minus_beta[:, 1:2])
        tv_term = wide("tv_term")
        nc.scalar.activation(tv_term[:], tv2[:], ACT.Copy, scale=alpha[:])

        v_factor = column("v_factor")
        nc.vector.tensor_scalar(v_factor[:], sum_y[:], inv_s, cross[:], ALU.mult, ALU.add)
        rest = wide("rest")
        nc.vector.scalar_tensor_tensor(rest[:], v, v_factor[:], y[:], ALU.mult, ALU.subtract)
        nc.vector.tensor_tensor(placed[:].indirect(offsets[:]), rest[:], tv_term[:], ALU.add)

        start = 0
        for n, width in enumerate(OUT_WIDTHS):
            cols = slice(start, start + width)
            result = held.tile([P, width], F32, name="result%d" % n)
            nc.vector.scalar_tensor_tensor(result[:], placed[:, cols], out_scale[:], base_sb[:, cols], ALU.mult, ALU.add)
            nc.sync.dma_start(out[:, cols], result[:])
            start = start + width
